import numpy as np
import ml_dtypes

BF16 = ml_dtypes.bfloat16


def bf(x):
    return np.asarray(x, np.float32).astype(BF16)


def f32(x):
    return np.asarray(x, np.float32)


def f64(x):
    return np.asarray(x).astype(np.float64)


def striped(idx):
    return np.concatenate([l.reshape(-1, 16).T for l in idx])


def rows(idx, k):
    return np.tile(np.repeat(idx, 16, axis=0), (k // (16 * 8), 1))


def look(tab, idx):
    return np.take_along_axis(f64(tab), rows(idx, len(tab)), axis=1)


K, S, V, N, M = 128, 2048, 2048, 2048, 512


def setup_inputs():
    return {"tab": f32(np.random.standard_normal((2, K, S))), "w": bf(np.random.standard_normal((K, M)) / np.sqrt(K)), "offs": striped(np.stack([np.random.permutation(S)[:N] for _ in range(8)]))}


def reference(tab, w, offs):
    idx = np.stack([g.T.reshape(-1) for g in np.split(offs, 8)])
    x = 1.0 / (1.0 + np.exp(-look(tab[0], idx))) * np.tanh(look(tab[1], idx))
    y = f64(w).T @ x
    return y

@@ -1,0 +1,44 @@
+import concourse.mybir as mybir
+
+ROWS, PLACES, PICKS, OUT_ROWS = 128, 2048, 2048, 512
+PIECE = 512
+GROUP = 16
+FLOPS = 2 * ROWS * OUT_ROWS * PICKS
+
+F32, BF16, U16 = mybir.dt.float32, mybir.dt.bfloat16, mybir.dt.uint16
+ACT = mybir.ActivationFunctionType
+
+
+def tile_lookup_cell_sigtanh_none_kernel(tc, tab, w, offs, out):
+    nc = tc.nc
+    blocks = OUT_ROWS // ROWS
+    with (
+        tc.tile_pool(name="held", bufs=1) as held,
+        tc.tile_pool(name="work", bufs=2) as work,
+        tc.tile_pool(name="staged", bufs=8) as staged,
+        tc.psum_pool(name="psum", bufs=8) as psum,
+    ):
+        offsets = held.tile([ROWS, PICKS // GROUP], U16)
+        gate_table = held.tile([ROWS, PLACES], F32)
+        state_table = held.tile([ROWS, PLACES], F32)
+        weights = held.tile([ROWS, OUT_ROWS], BF16)
+        nc.sync.dma_start(offsets[:], offs)
+        nc.sync.dma_start(gate_table[:], tab[0])
+        nc.sync.dma_start(state_table[:], tab[1])
+        nc.sync.dma_start(weights[:], w)
+
+        for piece in range(PICKS // PIECE):
+            picks = offsets[:, piece * PIECE // GROUP : (piece + 1) * PIECE // GROUP]
+            gate = work.tile([ROWS, PIECE], F32)
+            state = work.tile([ROWS, PIECE], F32)
+            x = work.tile([ROWS, PIECE], BF16)
+            nc.scalar.activation(gate[:], gate_table[:].indirect(picks), ACT.Sigmoid)
+            nc.scalar.activation(state[:], state_table[:].indirect(picks), ACT.Tanh)
+            nc.vector.tensor_mul(x[:], gate[:], state[:])
+            for block in range(blocks):
+                rows = slice(block * ROWS, (block + 1) * ROWS)
+                product = psum.tile([ROWS, PIECE], F32)
+                result = staged.tile([ROWS, PIECE], F32)
+                nc.tensor.matmul(product[:], weights[:, rows], x[:], start=True, stop=True)
+                nc.vector.tensor_copy(result[:], product[:])
+                nc.sync.dma_start(out[rows, piece * PIECE : (piece + 1) * PIECE], result[:])

@@ -12,10 +12,11 @@ ACT = mybir.ActivationFunctionType
 def tile_lookup_cell_sigtanh_none_kernel(tc, tab, w, offs, out):
     nc = tc.nc
     blocks = OUT_ROWS // ROWS
+    pieces = PICKS // PIECE
     with (
         tc.tile_pool(name="held", bufs=1) as held,
         tc.tile_pool(name="work", bufs=2) as work,
-        tc.tile_pool(name="staged", bufs=8) as staged,
+        tc.tile_pool(name="staged", bufs=16) as staged,
         tc.psum_pool(name="psum", bufs=8) as psum,
     ):
         offsets = held.tile([ROWS, PICKS // GROUP], U16)
@@ -27,18 +28,27 @@ def tile_lookup_cell_sigtanh_none_kernel(tc, tab, w, offs, out):
         nc.sync.dma_start(state_table[:], tab[1])
         nc.sync.dma_start(weights[:], w)
 
-        for piece in range(PICKS // PIECE):
+        warm_in = held.tile([ROWS, 8], F32)
+        warm_out = held.tile([ROWS, 8], F32)
+        nc.vector.memset(warm_in[:], 0.0)
+        nc.scalar.activation(warm_out[:], warm_in[:], ACT.Sigmoid)
+
+        for piece in range(pieces):
             picks = offsets[:, piece * PIECE // GROUP : (piece + 1) * PIECE // GROUP]
             gate = work.tile([ROWS, PIECE], F32)
             state = work.tile([ROWS, PIECE], F32)
             x = work.tile([ROWS, PIECE], BF16)
             nc.scalar.activation(gate[:], gate_table[:].indirect(picks), ACT.Sigmoid)
             nc.scalar.activation(state[:], state_table[:].indirect(picks), ACT.Tanh)
-            nc.vector.tensor_mul(x[:], gate[:], state[:])
+            multiplier = nc.vector if piece == 0 else nc.gpsimd
+            multiplier.tensor_mul(x[:], gate[:], state[:])
             for block in range(blocks):
                 rows = slice(block * ROWS, (block + 1) * ROWS)
                 product = psum.tile([ROWS, PIECE], F32)
                 result = staged.tile([ROWS, PIECE], F32)
                 nc.tensor.matmul(product[:], weights[:, rows], x[:], start=True, stop=True)
-                nc.vector.tensor_copy(result[:], product[:])
+                if piece == pieces - 1 and block % 2 == 1:
+                    nc.scalar.copy(result[:], product[:])
+                else:
+                    nc.vector.tensor_copy(result[:], product[:])
                 nc.sync.dma_start(out[rows, piece * PIECE : (piece + 1) * PIECE], result[:])

@@ -16,7 +16,8 @@ def tile_lookup_cell_sigtanh_none_kernel(tc, tab, w, offs, out):
     with (
         tc.tile_pool(name="held", bufs=1) as held,
         tc.tile_pool(name="work", bufs=2) as work,
-        tc.tile_pool(name="staged", bufs=16) as staged,
+        tc.tile_pool(name="cells", bufs=PICKS // PIECE) as cells,
+        tc.tile_pool(name="staged", bufs=17) as staged,
         tc.psum_pool(name="psum", bufs=8) as psum,
     ):
         offsets = held.tile([ROWS, PICKS // GROUP], U16)
@@ -33,22 +34,44 @@ def tile_lookup_cell_sigtanh_none_kernel(tc, tab, w, offs, out):
         nc.vector.memset(warm_in[:], 0.0)
         nc.scalar.activation(warm_out[:], warm_in[:], ACT.Sigmoid)
 
-        for piece in range(pieces):
+        whole = [slice(0, PIECE)]
+        halves = [slice(0, PIECE // 2), slice(PIECE // 2, PIECE)]
+
+        def look_up(piece):
             picks = offsets[:, piece * PIECE // GROUP : (piece + 1) * PIECE // GROUP]
             gate = work.tile([ROWS, PIECE], F32)
             state = work.tile([ROWS, PIECE], F32)
-            x = work.tile([ROWS, PIECE], BF16)
             nc.scalar.activation(gate[:], gate_table[:].indirect(picks), ACT.Sigmoid)
             nc.scalar.activation(state[:], state_table[:].indirect(picks), ACT.Tanh)
-            multiplier = nc.vector if piece == 0 else nc.gpsimd
-            multiplier.tensor_mul(x[:], gate[:], state[:])
-            for block in range(blocks):
+            return gate, state
+
+        def multiply(piece, gate, state):
+            x = cells.tile([ROWS, PIECE], BF16)
+            multiplier = nc.vector if piece in (0, pieces - 1) else nc.gpsimd
+            for span in halves if piece == 0 else whole:
+                multiplier.tensor_mul(x[:, span], gate[:, span], state[:, span])
+            return x
+
+        def dense(piece, x, block_range):
+            for block in block_range:
                 rows = slice(block * ROWS, (block + 1) * ROWS)
-                product = psum.tile([ROWS, PIECE], F32)
-                result = staged.tile([ROWS, PIECE], F32)
-                nc.tensor.matmul(product[:], weights[:, rows], x[:], start=True, stop=True)
-                if piece == pieces - 1 and block % 2 == 1:
-                    nc.scalar.copy(result[:], product[:])
-                else:
-                    nc.vector.tensor_copy(result[:], product[:])
-                nc.sync.dma_start(out[rows, piece * PIECE : (piece + 1) * PIECE], result[:])
+                for span in halves if piece == 0 and block == 0 else whole:
+                    width = span.stop - span.start
+                    product = psum.tile([ROWS, width], F32)
+                    result = staged.tile([ROWS, width], F32)
+                    nc.tensor.matmul(product[:], weights[:, rows], x[:, span], start=True, stop=True)
+                    if piece >= pieces - 2 and 0 < block < blocks - 1:
+                        nc.scalar.copy(result[:], product[:])
+                    else:
+                        nc.vector.tensor_copy(result[:], product[:])
+                    columns = slice(piece * PIECE + span.start, piece * PIECE + span.stop)
+                    nc.sync.dma_start(out[rows, columns], result[:])
+
+        x = multiply(0, *look_up(0))
+        for piece in range(pieces - 1):
+            following = look_up(piece + 1)
+            dense(piece, x, range(1))
+            next_x = multiply(piece + 1, *following)
+            dense(piece, x, range(1, blocks))
+            x = next_x
+        dense(pieces - 1, x, range(blocks))

import concourse.mybir as mybir

ROWS, PLACES, PICKS, OUT_ROWS = 128, 2048, 2048, 512
PIECE = 512
GROUP = 16
FLOPS = 2 * ROWS * OUT_ROWS * PICKS

F32, BF16, U16 = mybir.dt.float32, mybir.dt.bfloat16, mybir.dt.uint16
ACT = mybir.ActivationFunctionType


def tile_lookup_cell_sigtanh_none_kernel(tc, tab, w, offs, out):
    nc = tc.nc
    blocks = OUT_ROWS // ROWS
    pieces = PICKS // PIECE
    with (
        tc.tile_pool(name="held", bufs=1) as held,
        tc.tile_pool(name="work", bufs=2) as work,
        tc.tile_pool(name="cells", bufs=PICKS // PIECE) as cells,
        tc.tile_pool(name="staged", bufs=17) as staged,
        tc.psum_pool(name="psum", bufs=8) as psum,
    ):
        offsets = held.tile([ROWS, PICKS // GROUP], U16)
        gate_table = held.tile([ROWS, PLACES], F32)
        state_table = held.tile([ROWS, PLACES], F32)
        weights = held.tile([ROWS, OUT_ROWS], BF16)
        nc.sync.dma_start(offsets[:], offs)
        nc.sync.dma_start(gate_table[:], tab[0])
        nc.sync.dma_start(state_table[:], tab[1])
        nc.sync.dma_start(weights[:], w)

        warm_in = held.tile([ROWS, 8], F32)
        warm_out = held.tile([ROWS, 8], F32)
        nc.vector.memset(warm_in[:], 0.0)
        nc.scalar.activation(warm_out[:], warm_in[:], ACT.Sigmoid)

        whole = [slice(0, PIECE)]
        halves = [slice(0, PIECE // 2), slice(PIECE // 2, PIECE)]

        def look_up(piece):
            picks = offsets[:, piece * PIECE // GROUP : (piece + 1) * PIECE // GROUP]
            gate = work.tile([ROWS, PIECE], F32)
            state = work.tile([ROWS, PIECE], F32)
            nc.scalar.activation(gate[:], gate_table[:].indirect(picks), ACT.Sigmoid)
            nc.scalar.activation(state[:], state_table[:].indirect(picks), ACT.Tanh)
            return gate, state

        def multiply(piece, gate, state):
            x = cells.tile([ROWS, PIECE], BF16)
            multiplier = nc.vector if piece in (0, pieces - 1) else nc.gpsimd
            for span in halves if piece == 0 else whole:
                multiplier.tensor_mul(x[:, span], gate[:, span], state[:, span])
            return x

        def dense(piece, x, block_range):
            for block in block_range:
                rows = slice(block * ROWS, (block + 1) * ROWS)
                for span in halves if piece == 0 and block == 0 else whole:
                    width = span.stop - span.start
                    product = psum.tile([ROWS, width], F32)
                    result = staged.tile([ROWS, width], F32)
                    nc.tensor.matmul(product[:], weights[:, rows], x[:, span], start=True, stop=True)
                    if piece >= pieces - 2 and 0 < block < blocks - 1:
                        nc.scalar.copy(result[:], product[:])
                    else:
                        nc.vector.tensor_copy(result[:], product[:])
                    columns = slice(piece * PIECE + span.start, piece * PIECE + span.stop)
                    nc.sync.dma_start(out[rows, columns], result[:])

        x = multiply(0, *look_up(0))
        for piece in range(pieces - 1):
            following = look_up(piece + 1)
            dense(piece, x, range(1))
            next_x = multiply(piece + 1, *following)
            dense(piece, x, range(1, blocks))
            x = next_x
        dense(pieces - 1, x, range(blocks))
